import numpy as np
import ml_dtypes


def mxq(x, axis, fmt="e4m3"):
    dtype, down = {"e4m3": (ml_dtypes.float8_e4m3fn, 7), "e5m2": (ml_dtypes.float8_e5m2, 14)}[fmt]
    v = np.moveaxis(np.asarray(x, np.float32).astype(ml_dtypes.bfloat16).astype(np.float64), axis, -1)
    blocks = v.reshape(v.shape[:-1] + (-1, 32))
    amax = np.abs(blocks).max(-1, keepdims=True)
    byte = np.maximum(np.where(amax > 0, np.frexp(amax)[1] - 1 + 127, 0) - down, 1)
    scale = np.exp2(byte - 127.0)
    codes = (blocks / scale).astype(np.float32).astype(dtype).astype(np.float64)
    return np.moveaxis((codes * scale).reshape(v.shape), -1, axis)


WIDE = False


def mx_kscale(k):
    if not WIDE:
        return np.ones(k)
    levels = np.array([10, -10, 5, -5, 0])
    if k % 512:
        return np.exp2(np.random.permutation(np.resize(levels, k // 32))).repeat(32)
    a = np.empty((k // 512, 16))
    for p in range(k // 512):
        a[p, :8] = np.random.permutation(np.resize(levels, 8))
        for g in range(8):
            far = levels[np.abs(levels - a[p, g]) >= 10]
            a[p, g + 8] = far[np.random.randint(len(far))]
    return np.exp2(a.ravel()).repeat(32)


def f64(x):
    return np.asarray(x).astype(np.float64)


def striped(idx):
    return np.tile(idx.reshape(-1, 16).T, (8, 1)).astype(np.uint16)


def unstriped(offs):
    return offs[:16].T.reshape(-1).astype(np.int64)


def striped8(idx):
    return np.concatenate([x.reshape(-1, 16).T for x in idx]).astype(np.uint16)


def runs(offs, k):
    lists = np.stack([offs[16 * r : 16 * r + 16].T.reshape(-1) for r in range(8)]).astype(np.int64)
    return lists[np.arange(k) % 512 // 64]


def pack_weight(w):
    k, n = w.shape
    w = f64(np.asarray(w, np.float32).astype(ml_dtypes.bfloat16)).reshape(k // 32, 32, n)
    amax = np.abs(w).max(1)
    byte = np.clip(np.where(amax > 0, np.frexp(amax)[1] - 1 + 127 - 7, 1), 1, 254)
    scaled = (w * np.exp2(127.0 - byte)[:, None, :]).reshape(k, n).astype(np.float32)
    words = np.ascontiguousarray(scaled.reshape(k // 512, 128, 4, n).transpose(0, 1, 3, 2)).astype(ml_dtypes.float8_e4m3fn).view(np.uint8)
    return words, np.ascontiguousarray(byte.astype(np.uint8).reshape(k // 512, 16, n))


def unpack_weight(words, scales):
    g, p, n, _ = words.shape
    vals = np.ascontiguousarray(words).view(ml_dtypes.float8_e4m3fn).astype(np.float64) * np.repeat(np.exp2(scales.astype(np.float64) - 127.0), 8, axis=1)[..., None]
    return vals.transpose(0, 1, 3, 2).reshape(g * 512, n)


E2M1 = np.array([0.0, 0.5, 1.0, 1.5, 2.0, 3.0, 4.0, 6.0, -0.0, -0.5, -1.0, -1.5, -2.0, -3.0, -4.0, -6.0])


def pack_fp4(w):
    k, n = w.shape
    w = f64(np.asarray(w, np.float32).astype(ml_dtypes.bfloat16)).reshape(k // 32, 32, n)
    amax = np.abs(w).max(1)
    mant, ex = np.frexp(amax / 6.0)
    byte = np.clip(np.where(amax > 0, np.where(mant > 0.5, ex, ex - 1) + 127, 1), 1, 254)
    scaled = (w * np.exp2(127.0 - byte)[:, None, :]).reshape(k, n).astype(np.float32)
    c = np.ascontiguousarray(scaled.reshape(k // 512, 128, 4, n).transpose(0, 1, 3, 2)).astype(ml_dtypes.float4_e2m1fn).view(np.uint8) & 0xF
    words = (c[..., 0::2] | (c[..., 1::2] << 4)).reshape(k // 512, 128, 2 * n)
    return np.ascontiguousarray(words), np.ascontiguousarray(byte.astype(np.uint8).reshape(k // 512, 16, n))


def unpack_fp4(words, scales):
    g, _, n = scales.shape
    words = np.ascontiguousarray(words).reshape(g, 128, n, 2)
    nib = np.empty((g, 128, n, 4), np.uint8)
    nib[..., 0::2] = words & 0xF
    nib[..., 1::2] = words >> 4
    vals = E2M1[nib] * np.repeat(np.exp2(scales.astype(np.float64) - 127.0), 8, axis=1)[..., None]
    return vals.transpose(0, 1, 3, 2).reshape(g * 512, n)


K, T, S, N, G, H, U = 512, 1024, 256, 512, 2048, 512, 512


def setup_inputs():
    n = np.random.standard_normal
    s = mx_kscale(K)[:, None]
    u = mx_kscale(K)
    packed_xT = pack_weight(n((K, T)) * s)
    packed_dT = pack_weight(n((K, G)) / s)
    packed_w1 = pack_fp4(n((H, N)) / np.sqrt(H) / u[:, None])
    perm = np.random.permutation(U)
    return {
        "x_words": packed_xT[0],
        "x_scales": packed_xT[1],
        "d_words": packed_dT[0],
        "d_scales": packed_dT[1],
        "gn": (np.random.uniform(0.5, 1.5, (H, 1)) * u[:, None]).astype(np.float32),
        "w1_words": packed_w1[0],
        "w1_scales": packed_w1[1],
        "offs": striped8(np.random.randint(0, T, (8, S))),
        "ka": striped8(np.random.randint(0, G, (8, H))),
        "kb": striped8(np.random.randint(0, G, (8, H))),
        "n1": striped(perm[:S]),
        "n2": striped(perm[S:]),
        "n3": striped(np.random.permutation(S)),
    }


def reference(x_words, x_scales, d_words, d_scales, gn, w1_words, w1_scales, offs, ka, kb, n1, n2, n3):
    d_ka = unpack_weight(d_words, d_scales)[np.arange(K)[:, None], runs(ka, K)]
    xq = unpack_weight(x_words, x_scales)[np.arange(K)[:, None], runs(offs, K)]
    d_kb = unpack_weight(d_words, d_scales)[np.arange(K)[:, None], runs(kb, K)]
    h = 0.0625 * (d_ka.T @ xq + d_kb.T @ xq)
    z = f64(gn) * h
    h2 = unpack_fp4(w1_words, w1_scales).T @ mxq(z, 0, "e4m3")
    dn = np.minimum(h2, h2[:, unstriped(n3)])
    up = np.maximum(h2, h2[:, unstriped(n3)])
    ph = np.zeros((N, U))
    ph[:, unstriped(n1)] = up
    out = ph.copy()
    out[:, unstriped(n2)] = dn
    return out

@@ -1,0 +1,171 @@
+from contextlib import ExitStack
+
+import concourse.mybir as mybir
+
+K, T, S, N, G, H, U = 512, 1024, 256, 512, 2048, 512, 512
+FLOPS = 2 * (2 * K * H * S) + 2 * H * N * S
+
+F32 = mybir.dt.float32
+BF16 = mybir.dt.bfloat16
+I32 = mybir.dt.int32
+U32 = mybir.dt.uint32
+U16 = mybir.dt.uint16
+U8 = mybir.dt.uint8
+FP8X4 = mybir.dt.float8_e4m3fn_x4
+FP4X4 = mybir.dt.float4_e2m1fn_x4
+COPY = mybir.ActivationFunctionType.Copy
+ALU = mybir.AluOpType
+
+P = 128
+PACK = 4
+HALF = S // 2
+
+
+def tile_picked_haqipagmx_none_p_kernel(
+    tc, x_words, x_scales, d_words, d_scales, gn, w1_words, w1_scales, offs, ka, kb, n1, n2, n3, out
+):
+    nc = tc.nc
+    with ExitStack() as ctx:
+        sb = ctx.enter_context(tc.tile_pool(name="sb", bufs=1))
+        ps = ctx.enter_context(tc.psum_pool(name="ps", bufs=1))
+
+        def load_list(name, src):
+            tile = sb.tile(list(src.shape), U16, name=name)
+            nc.sync.dma_start(tile[:], src)
+            return tile
+
+        def load_scale_table(name, src, width):
+            tile = sb.tile([P, width], U8, name=name)
+            rows = src[0].bitcast(I32).unsqueeze(1).to_broadcast([16, 8, width // 4])
+            nc.sync.dma_start(tile[:].bitcast(I32), rows)
+            return tile
+
+        def load_word_table(name, src, width):
+            tile = sb.tile([P, width], U32, name=name)
+            nc.sync.dma_start(tile[:].bitcast(I32), src[0].rearrange("p n t -> p (n t)").bitcast(I32))
+            return tile
+
+        ka_list = load_list("ka_list", ka)
+        d_scale_table = load_scale_table("d_scale_table", d_scales, G)
+        kb_list = load_list("kb_list", kb)
+        offs_list = load_list("offs_list", offs)
+        x_scale_table = load_scale_table("x_scale_table", x_scales, T)
+        x_table = load_word_table("x_table", x_words, T)
+        d_table = load_word_table("d_table", d_words, G)
+
+        w1_codes = sb.tile([P, 2 * N], U8, align_bytes=64)
+        nc.sync.dma_start(w1_codes[:].bitcast(I32), w1_words[0].bitcast(I32))
+        n3_list = load_list("n3_list", n3)
+        n1_list = load_list("n1_list", n1)
+        n2_list = load_list("n2_list", n2)
+
+        gain = sb.tile([P, PACK], F32)
+        nc.scalar.dma_start(gain[:], gn.rearrange("(p t) o -> p (t o)", t=PACK))
+        w1_plane = sb.tile([P, N], U8, align_bytes=64)
+        nc.gpsimd.memset(w1_plane[:].bitcast(I32), 0)
+        for q in range(4):
+            nc.gpsimd.dma_start(
+                w1_plane[32 * q : 32 * q + 4, :].bitcast(I32), w1_scales[0, 4 * q : 4 * q + 4, :].bitcast(I32)
+            )
+        gain16 = sb.tile([P, PACK], F32)
+        nc.scalar.activation(gain16[:], gain[:], COPY, scale=0.0625)
+
+        picked_bytes = sb.tile([P, 2 * H + S], U8, align_bytes=64)
+        nc.vector.tensor_copy(picked_bytes[:, 0:H], d_scale_table[:].indirect(ka_list[:]))
+        nc.vector.tensor_copy(picked_bytes[:, H : 2 * H], d_scale_table[:].indirect(kb_list[:]))
+        nc.vector.tensor_copy(picked_bytes[:, 2 * H :], x_scale_table[:].indirect(offs_list[:]))
+        dealt_bytes = sb.tile([P, 2 * H + S], U8, align_bytes=64)
+        nc.vector.tensor_copy(
+            dealt_bytes[:, 0 : 2 * H].rearrange("p (t b i) -> p b t i", t=PACK, i=16),
+            picked_bytes[:, 0 : 2 * H].rearrange("p (b i t) -> p b t i", t=PACK, i=16),
+        )
+        nc.vector.tensor_copy(dealt_bytes[:, 2 * H :].bitcast(I32), picked_bytes[:, 2 * H :].bitcast(I32))
+        planes = sb.tile([P, 2 * H + S], U8, align_bytes=64)
+        nc.vector.memset(planes[:].bitcast(I32), 0)
+        for q in range(4):
+            queue = nc.sync if q % 2 == 0 else nc.scalar
+            queue.dma_start(
+                planes[32 * q : 32 * q + 4, :].bitcast(I32), dealt_bytes[32 * q : 32 * q + 32 : 8, :].bitcast(I32)
+            )
+
+        x_codes = sb.tile([P, S], U32, align_bytes=64)
+        nc.vector.tensor_copy(x_codes[:], x_table[:].indirect(offs_list[:]))
+        h_banks = [ps.tile([P, PACK, HALF], F32, name="h_bank%d" % half) for half in range(2)]
+        for s, k_list in enumerate((ka_list, kb_list)):
+            picked_words = sb.tile([P, H], U32, name="picked_words%d" % s)
+            nc.vector.tensor_copy(picked_words[:], d_table[:].indirect(k_list[:]))
+            d_codes = sb.tile([P, H], U32, align_bytes=64, name="d_codes%d" % s)
+            nc.vector.tensor_copy(
+                d_codes[:].rearrange("p (t b i) -> p b t i", t=PACK, i=4),
+                picked_words[:].rearrange("p (b i t) -> p b t i", t=PACK, i=4),
+            )
+            for half in range(2):
+                for t in range(PACK):
+                    d_col = (2 * t + s) * P
+                    x_col = 2 * H + half * HALF
+                    nc.tensor.matmul_mx(
+                        out=h_banks[half][:, t, :],
+                        lhsT=d_codes[:, t * P : (t + 1) * P].bitcast(FP8X4),
+                        lhsT_scale=planes[:, d_col : d_col + P],
+                        rhs=x_codes[:, half * HALF : (half + 1) * HALF].bitcast(FP8X4),
+                        rhs_scale=planes[:, x_col : x_col + HALF],
+                        start=(s == 0 and t == 0),
+                        stop=(s == 1 and t == PACK - 1),
+                    )
+
+        z_codes = sb.tile([P, S], U32, align_bytes=64)
+        z_plane = sb.tile([P, S], U8, align_bytes=64)
+        z_halves = []
+        for half in range(2):
+            z = sb.tile([P, HALF, PACK], BF16, align_bytes=64, name="z%d" % half)
+            nc.vector.tensor_tensor(
+                z[:],
+                h_banks[half][:].rearrange("p t j -> p j t"),
+                gain16[:].unsqueeze(1).to_broadcast([P, HALF, PACK]),
+                ALU.mult,
+            )
+            z_halves.append(z)
+        for half in range(2):
+            cols = slice(half * HALF, (half + 1) * HALF)
+            nc.vector.quantize_mx(
+                out=z_codes[:, cols].bitcast(FP8X4),
+                scales=z_plane[:, cols],
+                in_=z_halves[half][:].rearrange("p j t -> p (j t)"),
+            )
+
+        blocks = N // P
+        larger, smaller, pages = [], [], []
+        for b in range(blocks):
+            bank = ps.tile([P, S], F32, name="h2_bank%d" % b)
+            nc.tensor.matmul_mx(
+                out=bank[:],
+                lhsT=w1_codes[:, 2 * b * P : 2 * (b + 1) * P].bitcast(FP4X4),
+                lhsT_scale=w1_plane[:, b * P : (b + 1) * P],
+                rhs=z_codes[:].bitcast(FP8X4),
+                rhs_scale=z_plane[:],
+                start=True,
+                stop=True,
+            )
+            h2 = sb.tile([P, S], F32, name="h2_%d" % b)
+            nc.vector.tensor_copy(h2[:], bank[:])
+            partner = sb.tile([P, S], F32, name="partner%d" % b)
+            for half in range(2):
+                nc.scalar.activation(
+                    partner[:, half * HALF : (half + 1) * HALF],
+                    h2[:].indirect(n3_list[:, half * 8 : (half + 1) * 8]),
+                    COPY,
+                )
+            up = sb.tile([P, S], F32, name="up%d" % b)
+            nc.vector.tensor_tensor(up[:], h2[:], partner[:], ALU.max)
+            dn = sb.tile([P, S], F32, name="dn%d" % b)
+            nc.vector.tensor_tensor(dn[:], h2[:], partner[:], ALU.min)
+            larger.append(up)
+            smaller.append(dn)
+            pages.append(sb.tile([P, U], F32, name="page%d" % b))
+
+        for b in range(blocks + 1):
+            if b < blocks:
+                nc.scalar.activation(pages[b][:].indirect(n1_list[:]), larger[b][:], COPY)
+            if b > 0:
+                nc.scalar.activation(pages[b - 1][:].indirect(n2_list[:]), smaller[b - 1][:], COPY)
+                nc.sync.dma_start(out[(b - 1) * P : b * P, :], pages[b - 1][:])

@@ -1,6 +1,7 @@
 from contextlib import ExitStack
 
 import concourse.mybir as mybir
+from concourse.masks import make_identity
 
 K, T, S, N, G, H, U = 512, 1024, 256, 512, 2048, 512, 512
 FLOPS = 2 * (2 * K * H * S) + 2 * H * N * S
@@ -35,7 +36,7 @@ def tile_picked_haqipagmx_none_p_kernel(
             return tile
 
         def load_scale_table(name, src, width):
-            tile = sb.tile([P, width], U8, name=name)
+            tile = sb.tile([P, width], U8, name=name, tag=name, align_bytes=64)
             rows = src[0].bitcast(I32).unsqueeze(1).to_broadcast([16, 8, width // 4])
             nc.sync.dma_start(tile[:].bitcast(I32), rows)
             return tile
@@ -45,20 +46,20 @@ def tile_picked_haqipagmx_none_p_kernel(
             nc.sync.dma_start(tile[:].bitcast(I32), src[0].rearrange("p n t -> p (n t)").bitcast(I32))
             return tile
 
+        offs_list = load_list("offs_list", offs)
+        x_scale_table = load_scale_table("x_scale_table", x_scales, T)
         ka_list = load_list("ka_list", ka)
         d_scale_table = load_scale_table("d_scale_table", d_scales, G)
         kb_list = load_list("kb_list", kb)
-        offs_list = load_list("offs_list", offs)
-        x_scale_table = load_scale_table("x_scale_table", x_scales, T)
         x_table = load_word_table("x_table", x_words, T)
         d_table = load_word_table("d_table", d_words, G)
 
-        w1_codes = sb.tile([P, 2 * N], U8, align_bytes=64)
-        nc.sync.dma_start(w1_codes[:].bitcast(I32), w1_words[0].bitcast(I32))
         n3_list = load_list("n3_list", n3)
         n1_list = load_list("n1_list", n1)
         n2_list = load_list("n2_list", n2)
 
+        identity = sb.tile([P, P], F32)
+        make_identity(nc, identity[:])
         gain = sb.tile([P, PACK], F32)
         nc.scalar.dma_start(gain[:], gn.rearrange("(p t) o -> p (t o)", t=PACK))
         w1_plane = sb.tile([P, N], U8, align_bytes=64)
@@ -67,85 +68,98 @@ def tile_picked_haqipagmx_none_p_kernel(
             nc.gpsimd.dma_start(
                 w1_plane[32 * q : 32 * q + 4, :].bitcast(I32), w1_scales[0, 4 * q : 4 * q + 4, :].bitcast(I32)
             )
-        gain16 = sb.tile([P, PACK], F32)
-        nc.scalar.activation(gain16[:], gain[:], COPY, scale=0.0625)
+        gain_bank = ps.tile([P, PACK, P], F32, tag="turn0")
+        for t in range(PACK):
+            nc.tensor.transpose(gain_bank[:, t, :], gain[:, t : t + 1].to_broadcast([P, P]), identity[:])
+        gain16 = sb.tile([P, 2, P, 2], F32)
+        nc.scalar.activation(gain16[:], gain_bank[:].rearrange("j (u e) p -> j u p e", e=2), COPY, scale=0.0625)
 
-        picked_bytes = sb.tile([P, 2 * H + S], U8, align_bytes=64)
-        nc.vector.tensor_copy(picked_bytes[:, 0:H], d_scale_table[:].indirect(ka_list[:]))
-        nc.vector.tensor_copy(picked_bytes[:, H : 2 * H], d_scale_table[:].indirect(kb_list[:]))
-        nc.vector.tensor_copy(picked_bytes[:, 2 * H :], x_scale_table[:].indirect(offs_list[:]))
-        dealt_bytes = sb.tile([P, 2 * H + S], U8, align_bytes=64)
-        nc.vector.tensor_copy(
-            dealt_bytes[:, 0 : 2 * H].rearrange("p (t b i) -> p b t i", t=PACK, i=16),
-            picked_bytes[:, 0 : 2 * H].rearrange("p (b i t) -> p b t i", t=PACK, i=16),
-        )
-        nc.vector.tensor_copy(dealt_bytes[:, 2 * H :].bitcast(I32), picked_bytes[:, 2 * H :].bitcast(I32))
-        planes = sb.tile([P, 2 * H + S], U8, align_bytes=64)
-        nc.vector.memset(planes[:].bitcast(I32), 0)
-        for q in range(4):
-            queue = nc.sync if q % 2 == 0 else nc.scalar
-            queue.dma_start(
-                planes[32 * q : 32 * q + 4, :].bitcast(I32), dealt_bytes[32 * q : 32 * q + 32 : 8, :].bitcast(I32)
-            )
+        def move_rows(name, picked, width, queue):
+            plane = sb.tile([P, width], U8, align_bytes=64, name=name)
+            nc.vector.memset(plane[:].bitcast(I32), 0)
+            for q in range(4):
+                queue.dma_start(
+                    plane[32 * q : 32 * q + 4, :].bitcast(I32), picked[32 * q : 32 * q + 32 : 8, :].bitcast(I32)
+                )
+            return plane
+
+        picked_xa = sb.tile([P, S + H], U8, align_bytes=64)
+        nc.vector.tensor_copy(picked_xa[:, :S], x_scale_table[:].indirect(offs_list[:]))
+        nc.vector.tensor_copy(picked_xa[:, S:], d_scale_table[:].indirect(ka_list[:]))
+        plane_xa = move_rows("plane_xa", picked_xa, S + H, nc.scalar)
+        picked_b = sb.tile([P, H], U8, align_bytes=64)
+        nc.vector.tensor_copy(picked_b[:], d_scale_table[:].indirect(kb_list[:]))
+        plane_b = move_rows("plane_b", picked_b, H, nc.sync)
+
+        w1_codes = sb.tile([P, 2 * N], U8, align_bytes=64, tag="d_scale_table")
+        nc.sync.dma_start(w1_codes[:].bitcast(I32), w1_words[0].bitcast(I32))
 
         x_codes = sb.tile([P, S], U32, align_bytes=64)
         nc.vector.tensor_copy(x_codes[:], x_table[:].indirect(offs_list[:]))
-        h_banks = [ps.tile([P, PACK, HALF], F32, name="h_bank%d" % half) for half in range(2)]
-        for s, k_list in enumerate((ka_list, kb_list)):
-            picked_words = sb.tile([P, H], U32, name="picked_words%d" % s)
-            nc.vector.tensor_copy(picked_words[:], d_table[:].indirect(k_list[:]))
-            d_codes = sb.tile([P, H], U32, align_bytes=64, name="d_codes%d" % s)
-            nc.vector.tensor_copy(
-                d_codes[:].rearrange("p (t b i) -> p b t i", t=PACK, i=4),
-                picked_words[:].rearrange("p (b i t) -> p b t i", t=PACK, i=4),
+        a_codes = sb.tile([P, H], U32, align_bytes=64)
+        nc.vector.tensor_copy(a_codes[:], d_table[:].indirect(ka_list[:]))
+        b_codes = []
+        for part in range(2):
+            codes = sb.tile([P, S], U32, align_bytes=64, name="b_codes%d" % part)
+            nc.vector.tensor_copy(codes[:], d_table[:].indirect(kb_list[:, 16 * part : 16 * (part + 1)]))
+            b_codes.append(codes)
+
+        pieces = [(half, part) for part in range(2) for half in range(2)]
+        h_banks = {}
+        for half, part in pieces:
+            h_banks[half, part] = ps.tile([P, S], F32, name="h_bank", tag="acc%d" % (2 * part + half))
+        for first in (True, False):
+            for half, part in pieces:
+                tokens = slice(half * HALF, (half + 1) * HALF)
+                feats = slice(part * S, (part + 1) * S)
+                nc.tensor.matmul_mx(
+                    out=h_banks[half, part][:],
+                    lhsT=x_codes[:, tokens].bitcast(FP8X4),
+                    lhsT_scale=plane_xa[:, tokens],
+                    rhs=(a_codes[:, feats] if first else b_codes[part][:]).bitcast(FP8X4),
+                    rhs_scale=plane_xa[:, S + part * S : S + (part + 1) * S] if first else plane_b[:, feats],
+                    start=first,
+                    stop=not first,
+                )
+
+        z_rows = [sb.tile([P, 2, P, 2], BF16, name="z_rows%d" % half) for half in range(2)]
+        for half, part in pieces:
+            words = slice(64 * part, 64 * (part + 1))
+            nc.vector.tensor_tensor(
+                z_rows[half][:, :, words, :],
+                h_banks[half, part][:].rearrange("j (p u e) -> j u p e", u=2, e=2),
+                gain16[:, :, words, :],
+                ALU.mult,
             )
-            for half in range(2):
-                for t in range(PACK):
-                    d_col = (2 * t + s) * P
-                    x_col = 2 * H + half * HALF
-                    nc.tensor.matmul_mx(
-                        out=h_banks[half][:, t, :],
-                        lhsT=d_codes[:, t * P : (t + 1) * P].bitcast(FP8X4),
-                        lhsT_scale=planes[:, d_col : d_col + P],
-                        rhs=x_codes[:, half * HALF : (half + 1) * HALF].bitcast(FP8X4),
-                        rhs_scale=planes[:, x_col : x_col + HALF],
-                        start=(s == 0 and t == 0),
-                        stop=(s == 1 and t == PACK - 1),
-                    )
 
         z_codes = sb.tile([P, S], U32, align_bytes=64)
         z_plane = sb.tile([P, S], U8, align_bytes=64)
-        z_halves = []
         for half in range(2):
-            z = sb.tile([P, HALF, PACK], BF16, align_bytes=64, name="z%d" % half)
-            nc.vector.tensor_tensor(
-                z[:],
-                h_banks[half][:].rearrange("p t j -> p j t"),
-                gain16[:].unsqueeze(1).to_broadcast([P, HALF, PACK]),
-                ALU.mult,
+            pairs = z_rows[half][:].rearrange("j u p e -> j (u p e)").bitcast(F32)
+            turned = ps.tile([P, 2, HALF], F32, name="turned", tag="turn%d" % half)
+            for u in range(2):
+                nc.tensor.transpose(turned[:, u, :], pairs[:, u * P : (u + 1) * P], identity[:])
+            z = sb.tile([P, HALF * PACK], BF16, align_bytes=64, name="z%d" % half)
+            nc.scalar.copy(
+                z[:].bitcast(F32).rearrange("p (j u) -> p j u", u=2), turned[:].rearrange("p u j -> p j u")
             )
-            z_halves.append(z)
-        for half in range(2):
             cols = slice(half * HALF, (half + 1) * HALF)
-            nc.vector.quantize_mx(
-                out=z_codes[:, cols].bitcast(FP8X4),
-                scales=z_plane[:, cols],
-                in_=z_halves[half][:].rearrange("p j t -> p (j t)"),
-            )
+            nc.vector.quantize_mx(out=z_codes[:, cols].bitcast(FP8X4), scales=z_plane[:, cols], in_=z[:])
 
         blocks = N // P
         larger, smaller, pages = [], [], []
         for b in range(blocks):
-            bank = ps.tile([P, S], F32, name="h2_bank%d" % b)
-            nc.tensor.matmul_mx(
-                out=bank[:],
-                lhsT=w1_codes[:, 2 * b * P : 2 * (b + 1) * P].bitcast(FP4X4),
-                lhsT_scale=w1_plane[:, b * P : (b + 1) * P],
-                rhs=z_codes[:].bitcast(FP8X4),
-                rhs_scale=z_plane[:],
-                start=True,
-                stop=True,
-            )
+            bank = ps.tile([P, S], F32, name="h2_bank", tag="acc%d" % b)
+            for cols in (slice(0, HALF), slice(HALF, S)) if b == 0 else (slice(0, S),):
+                nc.tensor.matmul_mx(
+                    out=bank[:, cols],
+                    lhsT=w1_codes[:, 2 * b * P : 2 * (b + 1) * P].bitcast(FP4X4),
+                    lhsT_scale=w1_plane[:, b * P : (b + 1) * P],
+                    rhs=z_codes[:, cols].bitcast(FP8X4),
+                    rhs_scale=z_plane[:, cols],
+                    start=True,
+                    stop=True,
+                )
             h2 = sb.tile([P, S], F32, name="h2_%d" % b)
             nc.vector.tensor_copy(h2[:], bank[:])
             partner = sb.tile([P, S], F32, name="partner%d" % b)

@@ -96,13 +96,12 @@ def tile_picked_haqipagmx_none_p_kernel(
 
         x_codes = sb.tile([P, S], U32, align_bytes=64)
         nc.vector.tensor_copy(x_codes[:], x_table[:].indirect(offs_list[:]))
-        a_codes = sb.tile([P, H], U32, align_bytes=64)
-        nc.vector.tensor_copy(a_codes[:], d_table[:].indirect(ka_list[:]))
-        b_codes = []
-        for part in range(2):
-            codes = sb.tile([P, S], U32, align_bytes=64, name="b_codes%d" % part)
-            nc.vector.tensor_copy(codes[:], d_table[:].indirect(kb_list[:, 16 * part : 16 * (part + 1)]))
-            b_codes.append(codes)
+        d_codes = {}
+        for first, k_list in ((True, ka_list), (False, kb_list)):
+            for part in range(2):
+                codes = sb.tile([P, S], U32, align_bytes=64, name="d_codes%d%d" % (first, part))
+                nc.vector.tensor_copy(codes[:], d_table[:].indirect(k_list[:, 16 * part : 16 * (part + 1)]))
+                d_codes[first, part] = codes
 
         pieces = [(half, part) for part in range(2) for half in range(2)]
         h_banks = {}
@@ -116,7 +115,7 @@ def tile_picked_haqipagmx_none_p_kernel(
                     out=h_banks[half, part][:],
                     lhsT=x_codes[:, tokens].bitcast(FP8X4),
                     lhsT_scale=plane_xa[:, tokens],
-                    rhs=(a_codes[:, feats] if first else b_codes[part][:]).bitcast(FP8X4),
+                    rhs=d_codes[first, part][:].bitcast(FP8X4),
                     rhs_scale=plane_xa[:, S + part * S : S + (part + 1) * S] if first else plane_b[:, feats],
                     start=first,
                     stop=not first,
@@ -149,10 +148,15 @@ def tile_picked_haqipagmx_none_p_kernel(
         blocks = N // P
         larger, smaller, pages = [], [], []
         for b in range(blocks):
-            bank = ps.tile([P, S], F32, name="h2_bank", tag="acc%d" % b)
-            for cols in (slice(0, HALF), slice(HALF, S)) if b == 0 else (slice(0, S),):
+            h2 = sb.tile([P, S], F32, name="h2_%d" % b)
+            if b == 0:
+                spans = (("acc0", slice(0, HALF)), ("acc4", slice(HALF, S)))
+            else:
+                spans = (("acc%d" % b, slice(0, S)),)
+            for tag, cols in spans:
+                bank = ps.tile([P, cols.stop - cols.start], F32, name="h2_bank", tag=tag)
                 nc.tensor.matmul_mx(
-                    out=bank[:, cols],
+                    out=bank[:],
                     lhsT=w1_codes[:, 2 * b * P : 2 * (b + 1) * P].bitcast(FP4X4),
                     lhsT_scale=w1_plane[:, b * P : (b + 1) * P],
                     rhs=z_codes[:, cols].bitcast(FP8X4),
@@ -160,8 +164,7 @@ def tile_picked_haqipagmx_none_p_kernel(
                     start=True,
                     stop=True,
                 )
-            h2 = sb.tile([P, S], F32, name="h2_%d" % b)
-            nc.vector.tensor_copy(h2[:], bank[:])
+                nc.vector.tensor_copy(h2[:, cols], bank[:])
             partner = sb.tile([P, S], F32, name="partner%d" % b)
             for half in range(2):
                 nc.scalar.activation(

@@ -148,7 +148,8 @@ def tile_picked_haqipagmx_none_p_kernel(
         blocks = N // P
         larger, smaller, pages = [], [], []
         for b in range(blocks):
-            h2 = sb.tile([P, S], F32, name="h2_%d" % b)
+            h2 = sb.tile([P, S + 16], F32, name="h2_%d" % b)
+            nc.vector.memset(h2[:, S:], 0.0)
             if b == 0:
                 spans = (("acc0", slice(0, HALF)), ("acc4", slice(HALF, S)))
             else:
@@ -166,16 +167,11 @@ def tile_picked_haqipagmx_none_p_kernel(
                 )
                 nc.vector.tensor_copy(h2[:, cols], bank[:])
             partner = sb.tile([P, S], F32, name="partner%d" % b)
-            for half in range(2):
-                nc.scalar.activation(
-                    partner[:, half * HALF : (half + 1) * HALF],
-                    h2[:].indirect(n3_list[:, half * 8 : (half + 1) * 8]),
-                    COPY,
-                )
+            nc.scalar.activation(partner[:], h2[:].indirect(n3_list[:]), COPY)
             up = sb.tile([P, S], F32, name="up%d" % b)
-            nc.vector.tensor_tensor(up[:], h2[:], partner[:], ALU.max)
+            nc.vector.tensor_tensor(up[:], h2[:, :S], partner[:], ALU.max)
             dn = sb.tile([P, S], F32, name="dn%d" % b)
-            nc.vector.tensor_tensor(dn[:], h2[:], partner[:], ALU.min)
+            nc.vector.tensor_tensor(dn[:], h2[:, :S], partner[:], ALU.min)
             larger.append(up)
             smaller.append(dn)
             pages.append(sb.tile([P, U], F32, name="page%d" % b))

@@ -52,6 +52,8 @@ def tile_picked_haqipagmx_none_p_kernel(
         d_scale_table = load_scale_table("d_scale_table", d_scales, G)
         kb_list = load_list("kb_list", kb)
         x_table = load_word_table("x_table", x_words, T)
+        gain = sb.tile([P, PACK], F32)
+        nc.sync.dma_start(gain[:], gn.rearrange("(p t) o -> p (t o)", t=PACK))
         d_table = load_word_table("d_table", d_words, G)
 
         n3_list = load_list("n3_list", n3)
@@ -60,8 +62,6 @@ def tile_picked_haqipagmx_none_p_kernel(
 
         identity = sb.tile([P, P], F32)
         make_identity(nc, identity[:])
-        gain = sb.tile([P, PACK], F32)
-        nc.scalar.dma_start(gain[:], gn.rearrange("(p t) o -> p (t o)", t=PACK))
         w1_plane = sb.tile([P, N], U8, align_bytes=64)
         nc.gpsimd.memset(w1_plane[:].bitcast(I32), 0)
         for q in range(4):
@@ -181,4 +181,4 @@ def tile_picked_haqipagmx_none_p_kernel(
                 nc.scalar.activation(pages[b][:].indirect(n1_list[:]), larger[b][:], COPY)
             if b > 0:
                 nc.scalar.activation(pages[b - 1][:].indirect(n2_list[:]), smaller[b - 1][:], COPY)
-                nc.sync.dma_start(out[(b - 1) * P : b * P, :], pages[b - 1][:])
+                (nc.scalar if b == blocks else nc.sync).dma_start(out[(b - 1) * P : b * P, :], pages[b - 1][:])

from contextlib import ExitStack

import concourse.mybir as mybir
from concourse.masks import make_identity

K, T, S, N, G, H, U = 512, 1024, 256, 512, 2048, 512, 512
FLOPS = 2 * (2 * K * H * S) + 2 * H * N * S

F32 = mybir.dt.float32
BF16 = mybir.dt.bfloat16
I32 = mybir.dt.int32
U32 = mybir.dt.uint32
U16 = mybir.dt.uint16
U8 = mybir.dt.uint8
FP8X4 = mybir.dt.float8_e4m3fn_x4
FP4X4 = mybir.dt.float4_e2m1fn_x4
COPY = mybir.ActivationFunctionType.Copy
ALU = mybir.AluOpType

P = 128
PACK = 4
HALF = S // 2


def tile_picked_haqipagmx_none_p_kernel(
    tc, x_words, x_scales, d_words, d_scales, gn, w1_words, w1_scales, offs, ka, kb, n1, n2, n3, out
):
    nc = tc.nc
    with ExitStack() as ctx:
        sb = ctx.enter_context(tc.tile_pool(name="sb", bufs=1))
        ps = ctx.enter_context(tc.psum_pool(name="ps", bufs=1))

        def load_list(name, src):
            tile = sb.tile(list(src.shape), U16, name=name)
            nc.sync.dma_start(tile[:], src)
            return tile

        def load_scale_table(name, src, width):
            tile = sb.tile([P, width], U8, name=name, tag=name, align_bytes=64)
            rows = src[0].bitcast(I32).unsqueeze(1).to_broadcast([16, 8, width // 4])
            nc.sync.dma_start(tile[:].bitcast(I32), rows)
            return tile

        def load_word_table(name, src, width):
            tile = sb.tile([P, width], U32, name=name)
            nc.sync.dma_start(tile[:].bitcast(I32), src[0].rearrange("p n t -> p (n t)").bitcast(I32))
            return tile

        offs_list = load_list("offs_list", offs)
        x_scale_table = load_scale_table("x_scale_table", x_scales, T)
        ka_list = load_list("ka_list", ka)
        d_scale_table = load_scale_table("d_scale_table", d_scales, G)
        kb_list = load_list("kb_list", kb)
        x_table = load_word_table("x_table", x_words, T)
        gain = sb.tile([P, PACK], F32)
        nc.sync.dma_start(gain[:], gn.rearrange("(p t) o -> p (t o)", t=PACK))
        d_table = load_word_table("d_table", d_words, G)

        n3_list = load_list("n3_list", n3)
        n1_list = load_list("n1_list", n1)
        n2_list = load_list("n2_list", n2)

        identity = sb.tile([P, P], F32)
        make_identity(nc, identity[:])
        w1_plane = sb.tile([P, N], U8, align_bytes=64)
        nc.gpsimd.memset(w1_plane[:].bitcast(I32), 0)
        for q in range(4):
            nc.gpsimd.dma_start(
                w1_plane[32 * q : 32 * q + 4, :].bitcast(I32), w1_scales[0, 4 * q : 4 * q + 4, :].bitcast(I32)
            )
        gain_bank = ps.tile([P, PACK, P], F32, tag="turn0")
        for t in range(PACK):
            nc.tensor.transpose(gain_bank[:, t, :], gain[:, t : t + 1].to_broadcast([P, P]), identity[:])
        gain16 = sb.tile([P, 2, P, 2], F32)
        nc.scalar.activation(gain16[:], gain_bank[:].rearrange("j (u e) p -> j u p e", e=2), COPY, scale=0.0625)

        def move_rows(name, picked, width, queue):
            plane = sb.tile([P, width], U8, align_bytes=64, name=name)
            nc.vector.memset(plane[:].bitcast(I32), 0)
            for q in range(4):
                queue.dma_start(
                    plane[32 * q : 32 * q + 4, :].bitcast(I32), picked[32 * q : 32 * q + 32 : 8, :].bitcast(I32)
                )
            return plane

        picked_xa = sb.tile([P, S + H], U8, align_bytes=64)
        nc.vector.tensor_copy(picked_xa[:, :S], x_scale_table[:].indirect(offs_list[:]))
        nc.vector.tensor_copy(picked_xa[:, S:], d_scale_table[:].indirect(ka_list[:]))
        plane_xa = move_rows("plane_xa", picked_xa, S + H, nc.scalar)
        picked_b = sb.tile([P, H], U8, align_bytes=64)
        nc.vector.tensor_copy(picked_b[:], d_scale_table[:].indirect(kb_list[:]))
        plane_b = move_rows("plane_b", picked_b, H, nc.sync)

        w1_codes = sb.tile([P, 2 * N], U8, align_bytes=64, tag="d_scale_table")
        nc.sync.dma_start(w1_codes[:].bitcast(I32), w1_words[0].bitcast(I32))

        x_codes = sb.tile([P, S], U32, align_bytes=64)
        nc.vector.tensor_copy(x_codes[:], x_table[:].indirect(offs_list[:]))
        d_codes = {}
        for first, k_list in ((True, ka_list), (False, kb_list)):
            for part in range(2):
                codes = sb.tile([P, S], U32, align_bytes=64, name="d_codes%d%d" % (first, part))
                nc.vector.tensor_copy(codes[:], d_table[:].indirect(k_list[:, 16 * part : 16 * (part + 1)]))
                d_codes[first, part] = codes

        pieces = [(half, part) for part in range(2) for half in range(2)]
        h_banks = {}
        for half, part in pieces:
            h_banks[half, part] = ps.tile([P, S], F32, name="h_bank", tag="acc%d" % (2 * part + half))
        for first in (True, False):
            for half, part in pieces:
                tokens = slice(half * HALF, (half + 1) * HALF)
                feats = slice(part * S, (part + 1) * S)
                nc.tensor.matmul_mx(
                    out=h_banks[half, part][:],
                    lhsT=x_codes[:, tokens].bitcast(FP8X4),
                    lhsT_scale=plane_xa[:, tokens],
                    rhs=d_codes[first, part][:].bitcast(FP8X4),
                    rhs_scale=plane_xa[:, S + part * S : S + (part + 1) * S] if first else plane_b[:, feats],
                    start=first,
                    stop=not first,
                )

        z_rows = [sb.tile([P, 2, P, 2], BF16, name="z_rows%d" % half) for half in range(2)]
        for half, part in pieces:
            words = slice(64 * part, 64 * (part + 1))
            nc.vector.tensor_tensor(
                z_rows[half][:, :, words, :],
                h_banks[half, part][:].rearrange("j (p u e) -> j u p e", u=2, e=2),
                gain16[:, :, words, :],
                ALU.mult,
            )

        z_codes = sb.tile([P, S], U32, align_bytes=64)
        z_plane = sb.tile([P, S], U8, align_bytes=64)
        for half in range(2):
            pairs = z_rows[half][:].rearrange("j u p e -> j (u p e)").bitcast(F32)
            turned = ps.tile([P, 2, HALF], F32, name="turned", tag="turn%d" % half)
            for u in range(2):
                nc.tensor.transpose(turned[:, u, :], pairs[:, u * P : (u + 1) * P], identity[:])
            z = sb.tile([P, HALF * PACK], BF16, align_bytes=64, name="z%d" % half)
            nc.scalar.copy(
                z[:].bitcast(F32).rearrange("p (j u) -> p j u", u=2), turned[:].rearrange("p u j -> p j u")
            )
            cols = slice(half * HALF, (half + 1) * HALF)
            nc.vector.quantize_mx(out=z_codes[:, cols].bitcast(FP8X4), scales=z_plane[:, cols], in_=z[:])

        blocks = N // P
        larger, smaller, pages = [], [], []
        for b in range(blocks):
            h2 = sb.tile([P, S + 16], F32, name="h2_%d" % b)
            nc.vector.memset(h2[:, S:], 0.0)
            if b == 0:
                spans = (("acc0", slice(0, HALF)), ("acc4", slice(HALF, S)))
            else:
                spans = (("acc%d" % b, slice(0, S)),)
            for tag, cols in spans:
                bank = ps.tile([P, cols.stop - cols.start], F32, name="h2_bank", tag=tag)
                nc.tensor.matmul_mx(
                    out=bank[:],
                    lhsT=w1_codes[:, 2 * b * P : 2 * (b + 1) * P].bitcast(FP4X4),
                    lhsT_scale=w1_plane[:, b * P : (b + 1) * P],
                    rhs=z_codes[:, cols].bitcast(FP8X4),
                    rhs_scale=z_plane[:, cols],
                    start=True,
                    stop=True,
                )
                nc.vector.tensor_copy(h2[:, cols], bank[:])
            partner = sb.tile([P, S], F32, name="partner%d" % b)
            nc.scalar.activation(partner[:], h2[:].indirect(n3_list[:]), COPY)
            up = sb.tile([P, S], F32, name="up%d" % b)
            nc.vector.tensor_tensor(up[:], h2[:, :S], partner[:], ALU.max)
            dn = sb.tile([P, S], F32, name="dn%d" % b)
            nc.vector.tensor_tensor(dn[:], h2[:, :S], partner[:], ALU.min)
            larger.append(up)
            smaller.append(dn)
            pages.append(sb.tile([P, U], F32, name="page%d" % b))

        for b in range(blocks + 1):
            if b < blocks:
                nc.scalar.activation(pages[b][:].indirect(n1_list[:]), larger[b][:], COPY)
            if b > 0:
                nc.scalar.activation(pages[b - 1][:].indirect(n2_list[:]), smaller[b - 1][:], COPY)
                (nc.scalar if b == blocks else nc.sync).dma_start(out[(b - 1) * P : b * P, :], pages[b - 1][:])
